import numpy as np
import ml_dtypes


def mxq(x, axis, fmt="e4m3"):
    dtype, down = {"e4m3": (ml_dtypes.float8_e4m3fn, 7), "e5m2": (ml_dtypes.float8_e5m2, 14)}[fmt]
    v = np.moveaxis(np.asarray(x, np.float32).astype(ml_dtypes.bfloat16).astype(np.float64), axis, -1)
    blocks = v.reshape(v.shape[:-1] + (-1, 32))
    amax = np.abs(blocks).max(-1, keepdims=True)
    byte = np.maximum(np.where(amax > 0, np.frexp(amax)[1] - 1 + 127, 0) - down, 1)
    scale = np.exp2(byte - 127.0)
    codes = (blocks / scale).astype(np.float32).astype(dtype).astype(np.float64)
    return np.moveaxis((codes * scale).reshape(v.shape), -1, axis)


WIDE = False


def mx_kscale(k):
    if not WIDE:
        return np.ones(k)
    levels = np.array([30, -30])
    if k % 512:
        return np.exp2(np.random.permutation(np.resize(levels, k // 32))).repeat(32)
    a = np.empty((k // 512, 16))
    for p in range(k // 512):
        a[p, :8] = np.random.permutation(np.resize(levels, 8))
        for g in range(8):
            far = levels[np.abs(levels - a[p, g]) >= 10]
            a[p, g + 8] = far[np.random.randint(len(far))]
    return np.exp2(a.ravel()).repeat(32)


def f64(x):
    return np.asarray(x).astype(np.float64)


K, L, M, T = 1024, 1024, 512, 512


def setup_inputs():
    n = np.random.standard_normal
    s1 = mx_kscale(K)[:, None]
    s2 = mx_kscale(L)[:, None]
    m = np.exp(0.5 * n((1, T)))
    return {
        "w": (n((K, M)) / np.sqrt(K) / s1).astype(np.float32),
        "dy": (m * n((K, T)) * s1).astype(np.float32),
        "v": (n((L, M)) / np.sqrt(L) / s2).astype(np.float32),
        "e": (n((L, T)) * s2).astype(np.float32),
        "r": (n((512, 512))).astype(np.float32),
    }


def reference(w, dy, v, e, r):
    w_ = mxq(f64(w), 0, "e4m3")
    dy_ = mxq(f64(dy), 0, "e5m2")
    v_ = mxq(f64(v), 0, "e4m3")
    e_ = mxq(f64(e), 0, "e4m3")
    y = dy_.T @ w_ + e_.T @ v_
    return f64(r) + y

@@ -1,0 +1,86 @@
+from contextlib import ExitStack
+
+import concourse.mybir as mybir
+
+K, L, D, T = 1024, 1024, 512, 512
+
+F32 = mybir.dt.float32
+BF16 = mybir.dt.bfloat16
+U32 = mybir.dt.uint32
+U8 = mybir.dt.uint8
+E4M3 = mybir.dt.float8_e4m3fn_x4
+E5M2 = mybir.dt.float8_e5m2_x4
+
+P = 128
+PACK = 4
+K_PASS = P * PACK
+T_TILE = 128
+
+FLOPS = 2 * (K + L) * D * T
+
+
+def tile_mix_aux_tm_res_kernel(tc, w, dy, v, e, r, out):
+    nc = tc.nc
+    with ExitStack() as ctx:
+        keep = ctx.enter_context(tc.tile_pool(name="keep", bufs=1))
+        psum = ctx.enter_context(tc.psum_pool(name="psum", bufs=1))
+        ctx.enter_context(tc.manual_schedule())
+
+        operands = {"w": (w, E4M3), "dy": (dy, E5M2), "v": (v, E4M3), "e": (e, E4M3)}
+        pieces = [("w", 0, 0, 512), ("dy", 0, 0, 512), ("w", 1, 0, 512), ("dy", 1, 0, 512), ("v", 0, 0, 512), ("v", 1, 0, 512), ("e", 0, 0, 512), ("e", 1, 0, 256), ("e", 1, 256, 256)]
+        codes, planes = {}, {}
+        for name in operands:
+            for c in range(2):
+                codes[name, c] = keep.tile([P, 512], U32, name="codes_%s%d" % (name, c), align_bytes=64)
+                planes[name, c] = keep.tile([P, 512], U8, name="plane_%s%d" % (name, c), align_bytes=64)
+
+        raws = []
+        for name, c, first, width in pieces:
+            raw = keep.tile([P, PACK, width], F32, name="raw_%s%d_%d" % (name, c, first), align_bytes=64)
+            rows = operands[name][0][c * K_PASS : (c + 1) * K_PASS, first : first + width]
+            nc.sync.dma_start(out=raw[:], in_=rows.rearrange("(p j) x -> p j x", j=PACK))
+            raws.append(raw)
+        residuals = []
+        for m in range(T // T_TILE):
+            residual = keep.tile([P, D], F32, name="residual_%d" % m, align_bytes=64)
+            nc.sync.dma_start(out=residual[:], in_=r[m * T_TILE : (m + 1) * T_TILE, :])
+            residuals.append(residual)
+
+        sums = [psum.tile([T_TILE, D], F32, name="sum_%d" % m) for m in range(T // T_TILE)]
+
+        def multiply(stationary, moving, kind, c, m, start, stop):
+            t_cols = slice(m * T_TILE, (m + 1) * T_TILE)
+            nc.tensor.matmul_mx(
+                out=sums[m][:],
+                lhsT=codes[stationary, c][:, t_cols].bitcast(kind),
+                lhsT_scale=planes[stationary, c][:, t_cols],
+                rhs=codes[moving, c][:].bitcast(E4M3),
+                rhs_scale=planes[moving, c][:],
+                start=start,
+                stop=stop,
+            )
+
+        done = {}
+        for (name, c, first, width), raw in zip(pieces, raws):
+            grouped = keep.tile([P, width, PACK], BF16, name="grouped_%s%d_%d" % (name, c, first), align_bytes=64)
+            share = width * 5 // 8
+            source = raw[:].rearrange("p j x -> p x j")
+            nc.vector.tensor_copy(out=grouped[:, :share, :], in_=source[:, :share, :])
+            nc.scalar.copy(out=grouped[:, share:, :], in_=source[:, share:, :])
+            cols = slice(first, first + width)
+            nc.vector.quantize_mx(
+                out=codes[name, c][:, cols].bitcast(operands[name][1]),
+                scales=planes[name, c][:, cols],
+                in_=grouped[:].rearrange("p x j -> p (x j)"),
+            )
+            if name == "dy":
+                for m in range(4):
+                    multiply("dy", "w", E5M2, c, m, c == 0, False)
+            elif name == "e":
+                for m in range(first // T_TILE, (first + width) // T_TILE):
+                    multiply("e", "v", E4M3, c, m, False, c == 1)
+
+        for m in range(T // T_TILE):
+            result = keep.tile([P, D], F32, name="result_%d" % m, align_bytes=64)
+            nc.vector.tensor_tensor(out=result[:], in0=sums[m][:], in1=residuals[m][:], op=mybir.AluOpType.add)
+            nc.sync.dma_start(out=out[m * T_TILE : (m + 1) * T_TILE, :], in_=result[:])

@@ -27,60 +27,85 @@ def tile_mix_aux_tm_res_kernel(tc, w, dy, v, e, r, out):
         ctx.enter_context(tc.manual_schedule())
 
         operands = {"w": (w, E4M3), "dy": (dy, E5M2), "v": (v, E4M3), "e": (e, E4M3)}
-        pieces = [("w", 0, 0, 512), ("dy", 0, 0, 512), ("w", 1, 0, 512), ("dy", 1, 0, 512), ("v", 0, 0, 512), ("v", 1, 0, 512), ("e", 0, 0, 512), ("e", 1, 0, 256), ("e", 1, 256, 256)]
         codes, planes = {}, {}
         for name in operands:
             for c in range(2):
                 codes[name, c] = keep.tile([P, 512], U32, name="codes_%s%d" % (name, c), align_bytes=64)
                 planes[name, c] = keep.tile([P, 512], U8, name="plane_%s%d" % (name, c), align_bytes=64)
-
-        raws = []
-        for name, c, first, width in pieces:
-            raw = keep.tile([P, PACK, width], F32, name="raw_%s%d_%d" % (name, c, first), align_bytes=64)
-            rows = operands[name][0][c * K_PASS : (c + 1) * K_PASS, first : first + width]
-            nc.sync.dma_start(out=raw[:], in_=rows.rearrange("(p j) x -> p j x", j=PACK))
-            raws.append(raw)
-        residuals = []
-        for m in range(T // T_TILE):
-            residual = keep.tile([P, D], F32, name="residual_%d" % m, align_bytes=64)
-            nc.sync.dma_start(out=residual[:], in_=r[m * T_TILE : (m + 1) * T_TILE, :])
-            residuals.append(residual)
+        raws = {}
+        residuals = {}
+        for i, (name, c, n, first, width, queue) in enumerate([["w",0,1,0,512,0],["w",1,1,0,512,0],["v",0,1,0,512,0],["v",1,1,0,512,0],["dy",0,1,0,512,0],["dy",1,1,0,512,0],["e",0,1,0,512,0],["e",1,1,0,256,0],["e",1,1,256,256,0],["r",0,1,0,512,0],["r",1,1,0,512,0],["r",2,1,0,512,0],["r",3,1,0,512,0]]):
+            eng = nc.sync if queue == 0 else nc.scalar
+            if name == "r":
+                residual = keep.tile([P, n, D], F32, name="residual_%d" % i, align_bytes=64)
+                eng.dma_start(out=residual[:], in_=r[c * T_TILE : (c + n) * T_TILE, :].rearrange("(m p) x -> p m x", p=P))
+                for m in range(n):
+                    residuals[c + m] = residual[:, m, :]
+            else:
+                raw = keep.tile([P, n, PACK, width], F32, name="raw_%d" % i, align_bytes=64)
+                rows = operands[name][0][c * K_PASS : (c + n) * K_PASS, first : first + width]
+                if n == 1:
+                    eng.dma_start(out=raw[:, 0], in_=rows.rearrange("(p j) x -> p j x", j=PACK))
+                else:
+                    eng.dma_start(out=raw[:].rearrange("p c j x -> p c (j x)"), in_=rows.rearrange("(c p j) x -> p c (j x)", j=PACK, p=P))
+                for m in range(n):
+                    raws[name, c + m, first] = raw[:, m]
 
         sums = [psum.tile([T_TILE, D], F32, name="sum_%d" % m) for m in range(T // T_TILE)]
+        seen = {}
 
-        def multiply(stationary, moving, kind, c, m, start, stop):
+        def multiply(stationary, moving, kind, c, m):
             t_cols = slice(m * T_TILE, (m + 1) * T_TILE)
+            n = seen.get(m, 0)
+            seen[m] = n + 1
             nc.tensor.matmul_mx(
                 out=sums[m][:],
                 lhsT=codes[stationary, c][:, t_cols].bitcast(kind),
                 lhsT_scale=planes[stationary, c][:, t_cols],
                 rhs=codes[moving, c][:].bitcast(E4M3),
                 rhs_scale=planes[moving, c][:],
-                start=start,
-                stop=stop,
+                start=n == 0,
+                stop=n == 3,
             )
 
-        done = {}
-        for (name, c, first, width), raw in zip(pieces, raws):
-            grouped = keep.tile([P, width, PACK], BF16, name="grouped_%s%d_%d" % (name, c, first), align_bytes=64)
-            share = width * 5 // 8
-            source = raw[:].rearrange("p j x -> p x j")
-            nc.vector.tensor_copy(out=grouped[:, :share, :], in_=source[:, :share, :])
-            nc.scalar.copy(out=grouped[:, share:, :], in_=source[:, share:, :])
-            cols = slice(first, first + width)
-            nc.vector.quantize_mx(
-                out=codes[name, c][:, cols].bitcast(operands[name][1]),
-                scales=planes[name, c][:, cols],
-                in_=grouped[:].rearrange("p x j -> p (x j)"),
-            )
-            if name == "dy":
-                for m in range(4):
-                    multiply("dy", "w", E5M2, c, m, c == 0, False)
-            elif name == "e":
-                for m in range(first // T_TILE, (first + width) // T_TILE):
-                    multiply("e", "v", E4M3, c, m, False, c == 1)
-
-        for m in range(T // T_TILE):
-            result = keep.tile([P, D], F32, name="result_%d" % m, align_bytes=64)
-            nc.vector.tensor_tensor(out=result[:], in0=sums[m][:], in1=residuals[m][:], op=mybir.AluOpType.add)
-            nc.sync.dma_start(out=out[m * T_TILE : (m + 1) * T_TILE, :], in_=result[:])
+        grouped = {}
+        for step in [["c","w",0,0,512,320],["q","w",0,0,512],["c","w",1,0,512,320],["q","w",1,0,512],["c","v",0,0,512,320],["q","v",0,0,512],["c","v",1,0,512,320],["q","v",1,0,512],["c","dy",0,0,512,320],["q","dy",0,0,512],["dy",0,[0,1,2,3]],["c","dy",1,0,512,320],["q","dy",1,0,512],["dy",1,[0,1,2,3]],["c","e",0,0,512,320],["q","e",0,0,512],["e",0,[0,1,2,3]],["c","e",1,0,256,144],["q","e",1,0,256],["e",1,[0,1]],["c","e",1,256,256,144],["q","e",1,256,256],["e",1,[2,3]],["add",0,1],["add",1,1],["add",2,1],["add",3,2]]:
+            if step[0] == "c":
+                name, c, first, width, share = step[1:]
+                g = keep.tile([P, width, PACK], BF16, name="grouped_%s%d_%d" % (name, c, first), align_bytes=64)
+                grouped[name, c, first] = g
+                source = raws[name, c, first].rearrange("p j x -> p x j")
+                if share:
+                    nc.vector.tensor_copy(out=g[:, :share, :], in_=source[:, :share, :])
+                if share < width:
+                    nc.scalar.copy(out=g[:, share:, :], in_=source[:, share:, :])
+            elif step[0] == "q":
+                name, c, first, width = step[1:]
+                cols = slice(first, first + width)
+                nc.vector.quantize_mx(
+                    out=codes[name, c][:, cols].bitcast(operands[name][1]),
+                    scales=planes[name, c][:, cols],
+                    in_=grouped[name, c, first][:].rearrange("p x j -> p (x j)"),
+                )
+            elif step[0] == "dy":
+                for m in step[2]:
+                    multiply("dy", "w", E5M2, step[1], m)
+            elif step[0] == "e":
+                for m in step[2]:
+                    multiply("e", "v", E4M3, step[1], m)
+            elif step[0] == "gadd":
+                m = step[1]
+                plain = keep.tile([P, D], F32, name="plain_%d" % m, align_bytes=64)
+                nc.scalar.copy(out=plain[:], in_=sums[m][:])
+                result = keep.tile([P, D], F32, name="result_%d" % m, align_bytes=64)
+                nc.gpsimd.tensor_tensor(out=result[:], in0=plain[:], in1=residuals[m], op=mybir.AluOpType.add)
+                nc.scalar.dma_start(out=out[m * T_TILE : (m + 1) * T_TILE, :], in_=result[:])
+            elif step[0] == "add":
+                m, parts = step[1:]
+                width = D // parts
+                for h in range(parts):
+                    result = keep.tile([P, width], F32, name="result_%d_%d" % (m, h), align_bytes=64)
+                    cols = slice(h * width, (h + 1) * width)
+                    nc.vector.tensor_tensor(out=result[:], in0=sums[m][:, cols], in1=residuals[m][:, cols], op=mybir.AluOpType.add)
+                    eng = nc.scalar if h == 1 else nc.sync
+                    eng.dma_start(out=out[m * T_TILE : (m + 1) * T_TILE, cols], in_=result[:])

@@ -74,11 +74,14 @@ def tile_mix_aux_tm_res_kernel(tc, w, dy, v, e, r, out):
                 name, c, first, width, share = step[1:]
                 g = keep.tile([P, width, PACK], BF16, name="grouped_%s%d_%d" % (name, c, first), align_bytes=64)
                 grouped[name, c, first] = g
-                source = raws[name, c, first].rearrange("p j x -> p x j")
+                source = raws[name, c, first].rearrange("p j (x i) -> p x j i", i=4)
+                target = g[:].rearrange("p (x i) j -> p x j i", i=4)
+                share //= 4
+                width //= 4
                 if share:
-                    nc.vector.tensor_copy(out=g[:, :share, :], in_=source[:, :share, :])
+                    nc.vector.tensor_copy(out=target[:, :share], in_=source[:, :share])
                 if share < width:
-                    nc.scalar.copy(out=g[:, share:, :], in_=source[:, share:, :])
+                    nc.scalar.copy(out=target[:, share:], in_=source[:, share:])
             elif step[0] == "q":
                 name, c, first, width = step[1:]
                 cols = slice(first, first + width)

@@ -34,7 +34,7 @@ def tile_mix_aux_tm_res_kernel(tc, w, dy, v, e, r, out):
                 planes[name, c] = keep.tile([P, 512], U8, name="plane_%s%d" % (name, c), align_bytes=64)
         raws = {}
         residuals = {}
-        for i, (name, c, n, first, width, queue) in enumerate([["w",0,1,0,512,0],["w",1,1,0,512,0],["v",0,1,0,512,0],["v",1,1,0,512,0],["dy",0,1,0,512,0],["dy",1,1,0,512,0],["e",0,1,0,512,0],["e",1,1,0,256,0],["e",1,1,256,256,0],["r",0,1,0,512,0],["r",1,1,0,512,0],["r",2,1,0,512,0],["r",3,1,0,512,0]]):
+        for i, (name, c, n, first, width, queue) in enumerate([["w",0,1,0,512,0],["w",1,1,0,512,0],["v",0,1,0,512,0],["v",1,1,0,512,0],["dy",0,1,0,512,0],["dy",1,1,0,512,0],["e",0,1,0,512,0],["e",1,1,0,512,0],["r",0,2,0,512,0],["r",2,2,0,512,0]]):
             eng = nc.sync if queue == 0 else nc.scalar
             if name == "r":
                 residual = keep.tile([P, n, D], F32, name="residual_%d" % i, align_bytes=64)
@@ -69,12 +69,12 @@ def tile_mix_aux_tm_res_kernel(tc, w, dy, v, e, r, out):
             )
 
         grouped = {}
-        for step in [["c","w",0,0,512,320],["q","w",0,0,512],["c","w",1,0,512,320],["q","w",1,0,512],["c","v",0,0,512,320],["q","v",0,0,512],["c","v",1,0,512,320],["q","v",1,0,512],["c","dy",0,0,512,320],["q","dy",0,0,512],["dy",0,[0,1,2,3]],["c","dy",1,0,512,320],["q","dy",1,0,512],["dy",1,[0,1,2,3]],["c","e",0,0,512,320],["q","e",0,0,512],["e",0,[0,1,2,3]],["c","e",1,0,256,144],["q","e",1,0,256],["e",1,[0,1]],["c","e",1,256,256,144],["q","e",1,256,256],["e",1,[2,3]],["add",0,1],["add",1,1],["add",2,1],["add",3,2]]:
+        for step in [["c","w",0,0,512,320],["q","w",0,0,512],["c","w",1,0,512,320],["q","w",1,0,512],["c","v",0,0,512,320],["q","v",0,0,512],["c","v",1,0,512,320],["q","v",1,0,512],["c","dy",0,0,512,320],["q","dy",0,0,512],["dy",0,[0,1,2,3]],["c","dy",1,0,512,320],["q","dy",1,0,512],["dy",1,[0,1,2,3]],["c","e",0,0,512,320],["q","e",0,0,512],["e",0,[0,1,2,3]],["c","e",1,0,128,128],["c","e",1,256,128,0],["c","e",1,128,128,128],["c","e",1,384,128,0],["q","e",1,0,128],["e",1,[0]],["q","e",1,128,128],["e",1,[1]],["q","e",1,256,128],["e",1,[2]],["q","e",1,384,128],["e",1,[3]],["add",0,1],["add",1,1],["add",2,1],["add",3,2]]:
             if step[0] == "c":
                 name, c, first, width, share = step[1:]
                 g = keep.tile([P, width, PACK], BF16, name="grouped_%s%d_%d" % (name, c, first), align_bytes=64)
                 grouped[name, c, first] = g
-                source = raws[name, c, first].rearrange("p j (x i) -> p x j i", i=4)
+                source = raws[name, c, 0][:, :, first : first + width].rearrange("p j (x i) -> p x j i", i=4)
                 target = g[:].rearrange("p (x i) j -> p x j i", i=4)
                 share //= 4
                 width //= 4

from contextlib import ExitStack

import concourse.mybir as mybir

K, L, D, T = 1024, 1024, 512, 512

F32 = mybir.dt.float32
BF16 = mybir.dt.bfloat16
U32 = mybir.dt.uint32
U8 = mybir.dt.uint8
E4M3 = mybir.dt.float8_e4m3fn_x4
E5M2 = mybir.dt.float8_e5m2_x4

P = 128
PACK = 4
K_PASS = P * PACK
T_TILE = 128

FLOPS = 2 * (K + L) * D * T


def tile_mix_aux_tm_res_kernel(tc, w, dy, v, e, r, out):
    nc = tc.nc
    with ExitStack() as ctx:
        keep = ctx.enter_context(tc.tile_pool(name="keep", bufs=1))
        psum = ctx.enter_context(tc.psum_pool(name="psum", bufs=1))
        ctx.enter_context(tc.manual_schedule())

        operands = {"w": (w, E4M3), "dy": (dy, E5M2), "v": (v, E4M3), "e": (e, E4M3)}
        codes, planes = {}, {}
        for name in operands:
            for c in range(2):
                codes[name, c] = keep.tile([P, 512], U32, name="codes_%s%d" % (name, c), align_bytes=64)
                planes[name, c] = keep.tile([P, 512], U8, name="plane_%s%d" % (name, c), align_bytes=64)
        raws = {}
        residuals = {}
        for i, (name, c, n, first, width, queue) in enumerate([["w",0,1,0,512,0],["w",1,1,0,512,0],["v",0,1,0,512,0],["v",1,1,0,512,0],["dy",0,1,0,512,0],["dy",1,1,0,512,0],["e",0,1,0,512,0],["e",1,1,0,512,0],["r",0,2,0,512,0],["r",2,2,0,512,0]]):
            eng = nc.sync if queue == 0 else nc.scalar
            if name == "r":
                residual = keep.tile([P, n, D], F32, name="residual_%d" % i, align_bytes=64)
                eng.dma_start(out=residual[:], in_=r[c * T_TILE : (c + n) * T_TILE, :].rearrange("(m p) x -> p m x", p=P))
                for m in range(n):
                    residuals[c + m] = residual[:, m, :]
            else:
                raw = keep.tile([P, n, PACK, width], F32, name="raw_%d" % i, align_bytes=64)
                rows = operands[name][0][c * K_PASS : (c + n) * K_PASS, first : first + width]
                if n == 1:
                    eng.dma_start(out=raw[:, 0], in_=rows.rearrange("(p j) x -> p j x", j=PACK))
                else:
                    eng.dma_start(out=raw[:].rearrange("p c j x -> p c (j x)"), in_=rows.rearrange("(c p j) x -> p c (j x)", j=PACK, p=P))
                for m in range(n):
                    raws[name, c + m, first] = raw[:, m]

        sums = [psum.tile([T_TILE, D], F32, name="sum_%d" % m) for m in range(T // T_TILE)]
        seen = {}

        def multiply(stationary, moving, kind, c, m):
            t_cols = slice(m * T_TILE, (m + 1) * T_TILE)
            n = seen.get(m, 0)
            seen[m] = n + 1
            nc.tensor.matmul_mx(
                out=sums[m][:],
                lhsT=codes[stationary, c][:, t_cols].bitcast(kind),
                lhsT_scale=planes[stationary, c][:, t_cols],
                rhs=codes[moving, c][:].bitcast(E4M3),
                rhs_scale=planes[moving, c][:],
                start=n == 0,
                stop=n == 3,
            )

        grouped = {}
        for step in [["c","w",0,0,512,320],["q","w",0,0,512],["c","w",1,0,512,320],["q","w",1,0,512],["c","v",0,0,512,320],["q","v",0,0,512],["c","v",1,0,512,320],["q","v",1,0,512],["c","dy",0,0,512,320],["q","dy",0,0,512],["dy",0,[0,1,2,3]],["c","dy",1,0,512,320],["q","dy",1,0,512],["dy",1,[0,1,2,3]],["c","e",0,0,512,320],["q","e",0,0,512],["e",0,[0,1,2,3]],["c","e",1,0,128,128],["c","e",1,256,128,0],["c","e",1,128,128,128],["c","e",1,384,128,0],["q","e",1,0,128],["e",1,[0]],["q","e",1,128,128],["e",1,[1]],["q","e",1,256,128],["e",1,[2]],["q","e",1,384,128],["e",1,[3]],["add",0,1],["add",1,1],["add",2,1],["add",3,2]]:
            if step[0] == "c":
                name, c, first, width, share = step[1:]
                g = keep.tile([P, width, PACK], BF16, name="grouped_%s%d_%d" % (name, c, first), align_bytes=64)
                grouped[name, c, first] = g
                source = raws[name, c, 0][:, :, first : first + width].rearrange("p j (x i) -> p x j i", i=4)
                target = g[:].rearrange("p (x i) j -> p x j i", i=4)
                share //= 4
                width //= 4
                if share:
                    nc.vector.tensor_copy(out=target[:, :share], in_=source[:, :share])
                if share < width:
                    nc.scalar.copy(out=target[:, share:], in_=source[:, share:])
            elif step[0] == "q":
                name, c, first, width = step[1:]
                cols = slice(first, first + width)
                nc.vector.quantize_mx(
                    out=codes[name, c][:, cols].bitcast(operands[name][1]),
                    scales=planes[name, c][:, cols],
                    in_=grouped[name, c, first][:].rearrange("p x j -> p (x j)"),
                )
            elif step[0] == "dy":
                for m in step[2]:
                    multiply("dy", "w", E5M2, step[1], m)
            elif step[0] == "e":
                for m in step[2]:
                    multiply("e", "v", E4M3, step[1], m)
            elif step[0] == "gadd":
                m = step[1]
                plain = keep.tile([P, D], F32, name="plain_%d" % m, align_bytes=64)
                nc.scalar.copy(out=plain[:], in_=sums[m][:])
                result = keep.tile([P, D], F32, name="result_%d" % m, align_bytes=64)
                nc.gpsimd.tensor_tensor(out=result[:], in0=plain[:], in1=residuals[m], op=mybir.AluOpType.add)
                nc.scalar.dma_start(out=out[m * T_TILE : (m + 1) * T_TILE, :], in_=result[:])
            elif step[0] == "add":
                m, parts = step[1:]
                width = D // parts
                for h in range(parts):
                    result = keep.tile([P, width], F32, name="result_%d_%d" % (m, h), align_bytes=64)
                    cols = slice(h * width, (h + 1) * width)
                    nc.vector.tensor_tensor(out=result[:], in0=sums[m][:, cols], in1=residuals[m][:, cols], op=mybir.AluOpType.add)
                    eng = nc.scalar if h == 1 else nc.sync
                    eng.dma_start(out=out[m * T_TILE : (m + 1) * T_TILE, cols], in_=result[:])
